import numpy as np
import ml_dtypes


def mxq(x, axis, fmt="e4m3"):
    dtype, down = {"e4m3": (ml_dtypes.float8_e4m3fn, 7), "e5m2": (ml_dtypes.float8_e5m2, 14)}[fmt]
    v = np.moveaxis(np.asarray(x, np.float32).astype(ml_dtypes.bfloat16).astype(np.float64), axis, -1)
    blocks = v.reshape(v.shape[:-1] + (-1, 32))
    amax = np.abs(blocks).max(-1, keepdims=True)
    byte = np.maximum(np.where(amax > 0, np.frexp(amax)[1] - 1 + 127, 0) - down, 1)
    scale = np.exp2(byte - 127.0)
    codes = (blocks / scale).astype(np.float32).astype(dtype).astype(np.float64)
    return np.moveaxis((codes * scale).reshape(v.shape), -1, axis)


WIDE = False


def mx_kscale(k):
    if not WIDE:
        return np.ones(k)
    levels = np.array([10, -10, 5, -5, 0])
    if k % 512:
        return np.exp2(np.random.permutation(np.resize(levels, k // 32))).repeat(32)
    a = np.empty((k // 512, 16))
    for p in range(k // 512):
        a[p, :8] = np.random.permutation(np.resize(levels, 8))
        for g in range(8):
            far = levels[np.abs(levels - a[p, g]) >= 10]
            a[p, g + 8] = far[np.random.randint(len(far))]
    return np.exp2(a.ravel()).repeat(32)


def f64(x):
    return np.asarray(x).astype(np.float64)


def striped(idx):
    return np.tile(idx.reshape(-1, 16).T, (8, 1)).astype(np.uint16)


def unstriped(offs):
    return offs[:16].T.reshape(-1).astype(np.int64)


E2M1 = np.array([0.0, 0.5, 1.0, 1.5, 2.0, 3.0, 4.0, 6.0, -0.0, -0.5, -1.0, -1.5, -2.0, -3.0, -4.0, -6.0])


def pack_weight(w, fmt):
    k, n = w.shape
    w = f64(np.asarray(w, np.float32).astype(ml_dtypes.bfloat16)).reshape(k // 32, 32, n)
    amax = np.abs(w).max(1)
    if fmt == "e4m3":
        byte = np.frexp(amax)[1] - 1 + 127 - 7
    else:
        mant, ex = np.frexp(amax / 6.0)
        byte = np.where(mant > 0.5, ex, ex - 1) + 127
    byte = np.clip(np.where(amax > 0, byte, 1), 1, 254)
    scaled = (w * np.exp2(127.0 - byte)[:, None, :]).reshape(k, n).astype(np.float32)
    by_word = np.ascontiguousarray(scaled.reshape(k // 512, 128, 4, n).transpose(0, 1, 3, 2))
    if fmt == "e4m3":
        words = by_word.astype(ml_dtypes.float8_e4m3fn).view(np.uint8)
    else:
        c = by_word.astype(ml_dtypes.float4_e2m1fn).view(np.uint8) & 0xF
        words = (c[..., 0::2] | (c[..., 1::2] << 4)).reshape(k // 512, 128, 2 * n)
    return np.ascontiguousarray(words), np.ascontiguousarray(byte.astype(np.uint8).reshape(k // 512, 16, n))


def unpack_weight(words, scales, fmt):
    g, _, n = scales.shape
    words = np.ascontiguousarray(words).reshape(g, 128, n, -1)
    if fmt == "e4m3":
        vals = words.view(ml_dtypes.float8_e4m3fn).astype(np.float64)
    else:
        nib = np.empty((g, 128, n, 4), np.uint8)
        nib[..., 0::2] = words & 0xF
        nib[..., 1::2] = words >> 4
        vals = E2M1[nib]
    vals = vals * np.repeat(np.exp2(scales.astype(np.float64) - 127.0), 8, axis=1)[..., None]
    return vals.transpose(0, 1, 3, 2).reshape(g * 512, n)


def gelu(v):
    return 0.5 * v * (1.0 + np.tanh(np.sqrt(2.0 / np.pi) * (v + 0.044715 * v**3)))


K, T, S, P, P2, H, N = 512, 4096, 2048, 1024, 512, 1024, 512


def setup_inputs():
    n = np.random.standard_normal
    s = mx_kscale(K)[:, None]
    u = mx_kscale(H)[:, None]
    tab_words, tab_scales = pack_weight(n((K, T)) * s, "e4m3")
    w2_words, w2_scales = pack_weight(n((H, N)) / np.sqrt(H) / u, "e2m1")
    return {
        "tab_words": tab_words, "tab_scales": tab_scales,
        "offs": striped(np.random.permutation(T)[:S]),
        "pos1": striped(np.random.permutation(S)[:P]),
        "pos2": striped(np.random.permutation(S)[:P]),
        "pos3": striped(np.random.permutation(P)[:P2]),
        "pos4": striped(np.random.permutation(S)[:P2]),
        "w1": (n((K, H)) / np.sqrt(K) / s * u.T).astype(np.float32),
        "pingw": np.exp(0.3 * n(S)).astype(np.float32),
        "hopw": (0.7 * np.exp(0.3 * n(P))).astype(np.float32),
        "w2_words": w2_words, "w2_scales": w2_scales,
        "b": (0.6 * n(N)).astype(np.float32),
        "w3": (0.5 * n((H, N)) / np.sqrt(H) / u).astype(np.float32),
    }


def reference(tab_words, tab_scales, offs, pos1, pos2, pos3, pos4, w1, pingw, hopw,
              w2_words, w2_scales, b, w3):
    v = unpack_weight(tab_words, tab_scales, "e4m3")[:, unstriped(offs)]
    h = (mxq(f64(w1), 0, "e4m3").T @ v) * f64(pingw)[None, :]
    a1 = (h[:, unstriped(pos1)] - h[:, unstriped(pos2)]) * f64(hopw)[None, :]
    a2 = a1[:, unstriped(pos3)] + h[:, unstriped(pos4)]
    aq = mxq(a2, 0, "e4m3")
    w2 = unpack_weight(w2_words, w2_scales, "e2m1")
    bent = np.tanh((w2.T @ aq) + f64(b)[:, None])
    out = bent + (mxq(f64(w3), 0, "e4m3").T @ aq)
    return out

@@ -1,0 +1,259 @@
+from contextlib import ExitStack
+
+import concourse.mybir as mybir
+from concourse.masks import make_identity
+
+K, T, S, PAIRS, KEPT, H, N = 512, 4096, 2048, 1024, 512, 1024, 512
+FLOPS = 2 * K * H * S + 2 * 2 * H * N * KEPT
+
+F32 = mybir.dt.float32
+BF16 = mybir.dt.bfloat16
+I32 = mybir.dt.int32
+U32 = mybir.dt.uint32
+U16 = mybir.dt.uint16
+U8 = mybir.dt.uint8
+FP8X4 = mybir.dt.float8_e4m3fn_x4
+FP4X4 = mybir.dt.float4_e2m1fn_x4
+ALU = mybir.AluOpType
+ACT = mybir.ActivationFunctionType
+
+P = 128
+PACK = 4
+BANK = 512
+ROW_TILES = H // P
+PASSES = H // (P * PACK)
+PING_CHUNKS = S // BANK
+N_TILES = N // P
+KEPT_CHUNKS = (256, 128, 128)
+
+
+def tile_list_ping_hop_scores_kernel(
+    tc, tab_words, tab_scales, offs, pos1, pos2, pos3, pos4, w1, pingw, hopw,
+    w2_words, w2_scales, b, w3, out,
+):
+    nc = tc.nc
+    with ExitStack() as ctx:
+        lists = ctx.enter_context(tc.tile_pool(name="lists", bufs=1))
+        sb = ctx.enter_context(tc.tile_pool(name="sb", bufs=1))
+        psum = ctx.enter_context(tc.psum_pool(name="psum", bufs=1))
+
+        def held(name, shape, dtype, tag=None):
+            return sb.tile(shape, dtype, name=name, tag=tag or name, align_bytes=64)
+
+        def bank(index):
+            return psum.tile([P, BANK], F32, name="bank%d" % index, tag="bank%d" % index)
+
+        def load_list(name, source):
+            tile = lists.tile(list(source.shape), U16, name=name)
+            nc.sync.dma_start(tile[:], source)
+            return tile
+
+        idx = load_list("idx", offs)
+        p2 = load_list("p2", pos2)
+        p4 = load_list("p4", pos4)
+        p1 = load_list("p1", pos1)
+        p3 = load_list("p3", pos3)
+
+        def load_raw(rows):
+            raw = held("raw", [P, PACK, BANK], F32)
+            nc.sync.dma_start(raw[:], rows.rearrange("(p i) c -> p i c", i=PACK))
+            return raw
+
+        def quantise(name, values, columns, tag=None):
+            codes = held(name + "_codes", [P, columns], U32, tag)
+            scales = held(name + "_scales", [P, columns], U8)
+            nc.vector.quantize_mx(out=codes[:].bitcast(FP8X4), scales=scales[:], in_=values)
+            return codes, scales
+
+        def w1_codes_tag(tile_index):
+            return "w1_slot%d" % tile_index
+
+        w1q = {}
+
+        def prepare_w1(half, tag):
+            raw = load_raw(w1[:, half * BANK:(half + 1) * BANK])
+            rounded = held("w1_bf%d" % half, [P, BANK * PACK], BF16, tag)
+            src = raw[:].rearrange("p i (m t) -> p m t i", t=PACK)
+            dst = rounded[:].rearrange("p (t m i) -> p m t i", t=PACK, i=PACK)
+            for piece in range(2):
+                ms = slice(piece * P // 2, (piece + 1) * P // 2)
+                nc.scalar.copy(dst[:, ms], src[:, ms])
+            for t in range(PACK):
+                tile_index = half * PACK + t
+                w1q[tile_index] = quantise(
+                    "w1_%d" % tile_index, rounded[:, t * BANK:(t + 1) * BANK], P, w1_codes_tag(tile_index))
+
+        w3q = {}
+
+        def prepare_w3(a, tag):
+            raw = load_raw(w3[a * BANK:(a + 1) * BANK, :])
+            rounded = held("w3_bf%d" % a, [P, N * PACK], BF16, tag)
+            src = raw[:].rearrange("p i n -> p n i")
+            dst = rounded[:].rearrange("p (n i) -> p n i", i=PACK)
+            for piece in range(2):
+                ns = slice(piece * N // 2, (piece + 1) * N // 2)
+                nc.scalar.copy(dst[:, ns], src[:, ns])
+            w3q[a] = quantise("w3_%d" % a, rounded[:], N)
+
+        table_scales = held("table_scales", [P, T], U8)
+        nc.vector.memset(table_scales[:].bitcast(I32), 0)
+        for q in range(4):
+            nc.scalar.dma_start(table_scales[32 * q:32 * q + 4, :].bitcast(I32),
+                                tab_scales[0, 4 * q:4 * q + 4, :].bitcast(I32))
+        rows = held("rows", [P, P], F32)
+        nc.vector.memset(rows[:], 0.0)
+        nc.scalar.dma_start(rows[0:S // P, :], pingw.rearrange("(c p) -> c p", p=P))
+        nc.scalar.dma_start(rows[S // P:S // P + N_TILES, :], b.rearrange("(c p) -> c p", p=P))
+
+        prepare_w1(0, "w1_bf0")
+        table_words = held("table_words", [P, T], I32)
+        nc.sync.dma_start(table_words[:], tab_words[0].rearrange("p t i -> p (t i)").bitcast(I32))
+
+        ident = held("ident", [P, P], F32)
+        make_identity(nc, ident[:])
+        turned = bank(4)
+        nc.tensor.transpose(turned[:, 0:P], rows[:], ident[:])
+        columns = held("columns", [P, 32], F32)
+        nc.scalar.copy(columns[:], turned[:, 0:32])
+
+        hopw_rows = held("hopw_rows", [P, PAIRS], F32, "w1_bf0")
+        nc.sync.dma_start(hopw_rows[:], hopw.partition_broadcast(P))
+
+        picked_scales = held("picked_scales", [P, S], U8)
+        nc.vector.tensor_copy(picked_scales[:], table_scales[:].indirect(idx[:]))
+        picked_words = []
+        for c in range(PING_CHUNKS):
+            words = held("picked_words%d" % c, [P, BANK], U32)
+            nc.vector.tensor_copy(
+                words[:], table_words[:].bitcast(U32).indirect(idx[:, c * BANK // 16:(c + 1) * BANK // 16]))
+            picked_words.append(words)
+
+        def make_h(r):
+            codes, scales = w1q[r]
+            h = held("h%d" % r, [P, S], F32)
+            for c in range(PING_CHUNKS):
+                sums = bank(c)
+                for jj in range(PACK):
+                    cols = slice(jj * P, (jj + 1) * P)
+                    nc.tensor.matmul_mx(
+                        out=sums[:, cols],
+                        lhsT=picked_words[c][:, cols].bitcast(FP8X4),
+                        lhsT_scale=picked_scales[:, c * BANK + jj * P:c * BANK + (jj + 1) * P],
+                        rhs=codes[:].bitcast(FP8X4), rhs_scale=scales[:], start=True, stop=True)
+                weighted = held("weighted%d" % c, [P, BANK], F32)
+                for jj in range(PACK):
+                    cols = slice(jj * P, (jj + 1) * P)
+                    j_tile = c * PACK + jj
+                    nc.scalar.activation(weighted[:, cols], sums[:, cols], ACT.Copy,
+                                         scale=columns[:, j_tile:j_tile + 1])
+                back = bank(PING_CHUNKS + c)
+                for jj in range(PACK):
+                    cols = slice(jj * P, (jj + 1) * P)
+                    nc.tensor.transpose(back[:, cols], weighted[:, cols], ident[:])
+                nc.scalar.copy(h[:, c * BANK:(c + 1) * BANK], back[:])
+            return h
+
+        hops = {}
+        alibis = {}
+
+        def make_hops(r, h):
+            second = held("second%d" % (r % 2), [P, PAIRS], F32)
+            nc.vector.tensor_copy(second[:], h[:].indirect(p2[:]))
+            alibis[r] = held("alibi%d" % r, [P, KEPT], F32)
+            nc.vector.tensor_copy(alibis[r][:], h[:].indirect(p4[:]))
+            diff = held("diff%d" % (r % 2), [P, PAIRS], F32)
+            nc.vector.tensor_tensor(diff[:], h[:].indirect(p1[:]), second[:], ALU.subtract)
+            return diff
+
+        def weight_hops(r, diff):
+            engine = nc.vector if r == ROW_TILES - 1 else nc.gpsimd
+            hops[r] = held("hops%d" % (r % PACK), [P, PAIRS], F32)
+            engine.tensor_tensor(hops[r][:], diff[:], hopw_rows[:], ALU.mult)
+
+        def keep_hops(r, dst, j0, width):
+            nc.vector.tensor_tensor(dst, hops[r][:].indirect(p3[:, j0 // 16:(j0 + width) // 16]),
+                                    alibis[r][:, j0:j0 + width], ALU.add)
+
+        def round_kept(copy, name, planes, width, tag=None):
+            rounded = held(name, [P, width * PACK], BF16, tag)
+            copy(rounded[:].rearrange("p (j t) -> p j t", t=PACK), planes.rearrange("p (t j) -> p j t", t=PACK))
+            return rounded
+
+        w2w = None
+        w2s = None
+        kept0 = None
+        a2q0 = None
+        for r in range(ROW_TILES):
+            h = make_h(r)
+            if r == 0:
+                w2w = held("w2w", [P, PASSES, 2 * N], U8, w1_codes_tag(0))
+                nc.sync.dma_start(w2w[:].bitcast(I32), w2_words.rearrange("a p c -> p a c").bitcast(I32))
+            if r == 1:
+                prepare_w1(1, w1_codes_tag(1))
+            if r == 2:
+                w2s = held("w2s", [P, PASSES, N], U8, w1_codes_tag(2))
+                nc.gpsimd.memset(w2s[:].bitcast(I32), 0)
+                for q in range(4):
+                    nc.sync.dma_start(w2s[32 * q:32 * q + 4].bitcast(I32),
+                                      w2_scales[:, 4 * q:4 * q + 4, :].rearrange("a q c -> q a c").bitcast(I32))
+            if r == 4:
+                prepare_w3(0, w1_codes_tag(4))
+            if r == 7:
+                prepare_w3(1, w1_codes_tag(7))
+            diff = make_hops(r, h)
+            if r == PACK:
+                kept0 = held("kept0", [P, PACK * KEPT], F32, "h%d" % r)
+                for t in (1, 2, 3, 0):
+                    keep_hops(t, kept0[:, t * KEPT:(t + 1) * KEPT], 0, KEPT)
+            if r == 6:
+                a2q0 = quantise("a2_0", round_kept(nc.scalar.copy, "a2_bf0", kept0[:], KEPT, w1_codes_tag(6))[:], KEPT)
+            weight_hops(r, diff)
+
+        def products(acc, first_tile, tiles, width, a, moving, j0, start, stop):
+            codes, scales = moving
+            cols = slice(j0, j0 + width)
+            for u in range(tiles):
+                n0 = (first_tile + u) * P
+                nc.tensor.matmul_mx(
+                    out=acc[:, 2 * u * width:(2 * u + 1) * width],
+                    lhsT=w2w[:, a, 2 * n0:2 * (n0 + P)].bitcast(FP4X4), lhsT_scale=w2s[:, a, n0:n0 + P],
+                    rhs=codes[:, cols].bitcast(FP8X4), rhs_scale=scales[:, cols],
+                    start=start and u == 0, stop=False)
+                nc.tensor.matmul_mx(
+                    out=acc[:, (2 * u + 1) * width:(2 * u + 2) * width],
+                    lhsT=w3q[a][0][:, n0:n0 + P].bitcast(FP8X4), lhsT_scale=w3q[a][1][:, n0:n0 + P],
+                    rhs=codes[:, cols].bitcast(FP8X4), rhs_scale=scales[:, cols],
+                    start=False, stop=stop and u == tiles - 1)
+
+        starts = [sum(KEPT_CHUNKS[:k]) for k in range(len(KEPT_CHUNKS))]
+        accs = {}
+        next_bank = 0
+        for j0, width in zip(starts, KEPT_CHUNKS):
+            tiles = BANK // (2 * width)
+            for first_tile in range(0, N_TILES, tiles):
+                accs[j0, first_tile] = bank(next_bank)
+                next_bank = next_bank + 1
+                products(accs[j0, first_tile], first_tile, tiles, width, 0, a2q0, j0, True, False)
+
+        kept1 = held("kept1", [P, PACK * KEPT], F32, "h%d" % (ROW_TILES - 1))
+        out_view = out.rearrange("(i p) j -> p i j", p=P)
+        for j0, width in zip(starts, KEPT_CHUNKS):
+            planes = kept1[:, PACK * j0:PACK * (j0 + width)]
+            for t in range(PACK):
+                keep_hops(PACK + t, planes[:, t * width:(t + 1) * width], j0, width)
+            copy = nc.vector.tensor_copy if j0 == starts[-1] else nc.scalar.copy
+            rounded = round_kept(copy, "a2_bf1_%d" % j0, planes, width)
+            moving = quantise("a2_1_%d" % j0, rounded[:], width)
+            tiles = BANK // (2 * width)
+            for first_tile in range(0, N_TILES, tiles):
+                acc = accs[j0, first_tile]
+                products(acc, first_tile, tiles, width, 1, moving, 0, False, True)
+                bent = held("bent_%d_%d" % (j0, first_tile), [P, tiles, width], F32)
+                for u in range(tiles):
+                    n_tile = S // P + first_tile + u
+                    nc.scalar.activation(bent[:, u, :], acc[:, 2 * u * width:(2 * u + 1) * width], ACT.Tanh,
+                                         bias=columns[:, n_tile:n_tile + 1])
+                result = held("result_%d_%d" % (j0, first_tile), [P, tiles, width], F32)
+                straight = acc[:].rearrange("p (u s w) -> p u s w", s=2, w=width)[:, :, 1, :]
+                nc.vector.tensor_tensor(result[:], straight, bent[:], ALU.add)
+                nc.sync.dma_start(out_view[:, first_tile:first_tile + tiles, j0:j0 + width], result[:])

@@ -24,7 +24,8 @@ ROW_TILES = H // P
 PASSES = H // (P * PACK)
 PING_CHUNKS = S // BANK
 N_TILES = N // P
-KEPT_CHUNKS = (256, 128, 128)
+KEPT_CHUNK = 128
+KEPT_CHUNKS = KEPT // KEPT_CHUNK
 
 
 def tile_list_ping_hop_scores_kernel(
@@ -40,38 +41,45 @@ def tile_list_ping_hop_scores_kernel(
         def held(name, shape, dtype, tag=None):
             return sb.tile(shape, dtype, name=name, tag=tag or name, align_bytes=64)
 
-        def bank(index):
-            return psum.tile([P, BANK], F32, name="bank%d" % index, tag="bank%d" % index)
+        def banks(parity, count=PING_CHUNKS):
+            names = ["bank%d" % (parity * PING_CHUNKS + c) for c in range(count)]
+            return [psum.tile([P, BANK], F32, name=name, tag=name)[:] for name in names]
 
         def load_list(name, source):
             tile = lists.tile(list(source.shape), U16, name=name)
             nc.sync.dma_start(tile[:], source)
             return tile
 
+        rows = held("rows", [P, P], F32)
+        nc.gpsimd.memset(rows[:], 0.0)
         idx = load_list("idx", offs)
+        table_scales = held("table_scales", [P, T], U8)
+        nc.sync.dma_start(table_scales[:].bitcast(I32),
+                          tab_scales[0].bitcast(I32).unsqueeze(1).to_broadcast([16, 8, T // 4]))
         p2 = load_list("p2", pos2)
         p4 = load_list("p4", pos4)
         p1 = load_list("p1", pos1)
         p3 = load_list("p3", pos3)
+        nc.sync.dma_start(rows[0:S // P, :], pingw.rearrange("(c p) -> c p", p=P))
 
-        def load_raw(rows):
-            raw = held("raw", [P, PACK, BANK], F32)
+        def load_raw(rows, tag):
+            raw = held("raw", [P, PACK, BANK], F32, tag)
             nc.sync.dma_start(raw[:], rows.rearrange("(p i) c -> p i c", i=PACK))
             return raw
 
-        def quantise(name, values, columns, tag=None):
-            codes = held(name + "_codes", [P, columns], U32, tag)
+        def quantise(name, values, columns):
+            codes = held(name + "_codes", [P, columns], U32)
             scales = held(name + "_scales", [P, columns], U8)
             nc.vector.quantize_mx(out=codes[:].bitcast(FP8X4), scales=scales[:], in_=values)
             return codes, scales
 
         def w1_codes_tag(tile_index):
-            return "w1_slot%d" % tile_index
+            return "w1_%d_codes" % tile_index
 
         w1q = {}
 
-        def prepare_w1(half, tag):
-            raw = load_raw(w1[:, half * BANK:(half + 1) * BANK])
+        def prepare_w1(half, raw_tag, tag):
+            raw = load_raw(w1[:, half * BANK:(half + 1) * BANK], raw_tag)
             rounded = held("w1_bf%d" % half, [P, BANK * PACK], BF16, tag)
             src = raw[:].rearrange("p i (m t) -> p m t i", t=PACK)
             dst = rounded[:].rearrange("p (t m i) -> p m t i", t=PACK, i=PACK)
@@ -80,13 +88,12 @@ def tile_list_ping_hop_scores_kernel(
                 nc.scalar.copy(dst[:, ms], src[:, ms])
             for t in range(PACK):
                 tile_index = half * PACK + t
-                w1q[tile_index] = quantise(
-                    "w1_%d" % tile_index, rounded[:, t * BANK:(t + 1) * BANK], P, w1_codes_tag(tile_index))
+                w1q[tile_index] = quantise("w1_%d" % tile_index, rounded[:, t * BANK:(t + 1) * BANK], P)
 
         w3q = {}
 
         def prepare_w3(a, tag):
-            raw = load_raw(w3[a * BANK:(a + 1) * BANK, :])
+            raw = load_raw(w3[a * BANK:(a + 1) * BANK, :], "w1_bf0")
             rounded = held("w3_bf%d" % a, [P, N * PACK], BF16, tag)
             src = raw[:].rearrange("p i n -> p n i")
             dst = rounded[:].rearrange("p (n i) -> p n i", i=PACK)
@@ -95,32 +102,31 @@ def tile_list_ping_hop_scores_kernel(
                 nc.scalar.copy(dst[:, ns], src[:, ns])
             w3q[a] = quantise("w3_%d" % a, rounded[:], N)
 
-        table_scales = held("table_scales", [P, T], U8)
-        nc.vector.memset(table_scales[:].bitcast(I32), 0)
-        for q in range(4):
-            nc.scalar.dma_start(table_scales[32 * q:32 * q + 4, :].bitcast(I32),
-                                tab_scales[0, 4 * q:4 * q + 4, :].bitcast(I32))
-        rows = held("rows", [P, P], F32)
-        nc.vector.memset(rows[:], 0.0)
-        nc.scalar.dma_start(rows[0:S // P, :], pingw.rearrange("(c p) -> c p", p=P))
-        nc.scalar.dma_start(rows[S // P:S // P + N_TILES, :], b.rearrange("(c p) -> c p", p=P))
-
-        prepare_w1(0, "w1_bf0")
+        prepare_w1(0, "raw", "w1_bf0")
         table_words = held("table_words", [P, T], I32)
         nc.sync.dma_start(table_words[:], tab_words[0].rearrange("p t i -> p (t i)").bitcast(I32))
 
         ident = held("ident", [P, P], F32)
         make_identity(nc, ident[:])
-        turned = bank(4)
-        nc.tensor.transpose(turned[:, 0:P], rows[:], ident[:])
-        columns = held("columns", [P, 32], F32)
-        nc.scalar.copy(columns[:], turned[:, 0:32])
+        turned = banks(1, 1)
+        nc.tensor.transpose(turned[0][:, 0:P], rows[:], ident[:])
+        columns = held("columns", [P, S // P], F32)
+        nc.scalar.copy(columns[:], turned[0][:, 0:S // P])
+        spread = banks(0)
+        pingw_rows = held("pingw_rows", [P, PING_CHUNKS, BANK], F32)
+        for c in range(PING_CHUNKS):
+            for jj in range(PACK):
+                j_tile = c * PACK + jj
+                nc.tensor.transpose(spread[c][:, jj * P:(jj + 1) * P],
+                                    columns[:, j_tile:j_tile + 1].to_broadcast([P, P]), ident[:])
+            nc.scalar.copy(pingw_rows[:, c, :], spread[c])
 
-        hopw_rows = held("hopw_rows", [P, PAIRS], F32, "w1_bf0")
-        nc.sync.dma_start(hopw_rows[:], hopw.partition_broadcast(P))
-
+        gathered_scales = held("gathered_scales", [P, S], U8)
+        nc.vector.tensor_copy(gathered_scales[:], table_scales[:].indirect(idx[:]))
         picked_scales = held("picked_scales", [P, S], U8)
-        nc.vector.tensor_copy(picked_scales[:], table_scales[:].indirect(idx[:]))
+        nc.gpsimd.memset(picked_scales[:].bitcast(I32), 0)
+        for q in range(4):
+            nc.sync.dma_start(picked_scales[q:P:32, :].bitcast(I32), gathered_scales[8 * q:P:32, :].bitcast(I32))
         picked_words = []
         for c in range(PING_CHUNKS):
             words = held("picked_words%d" % c, [P, BANK], U32)
@@ -128,29 +134,48 @@ def tile_list_ping_hop_scores_kernel(
                 words[:], table_words[:].bitcast(U32).indirect(idx[:, c * BANK // 16:(c + 1) * BANK // 16]))
             picked_words.append(words)
 
+        def make_first_h():
+            codes, scales = w1q[0]
+            h = held("h0", [P, S], F32)
+            sums = banks(0)
+            for c in range(PING_CHUNKS):
+                cols = slice(c * BANK, (c + 1) * BANK)
+                nc.tensor.matmul_mx(
+                    out=sums[c], lhsT=codes[:].bitcast(FP8X4), lhsT_scale=scales[:],
+                    rhs=picked_words[c][:].bitcast(FP8X4), rhs_scale=picked_scales[:, cols],
+                    start=True, stop=True)
+                if c < PING_CHUNKS // 2:
+                    plain = held("plain%d" % c, [P, BANK], F32)
+                    nc.scalar.copy(plain[:], sums[c])
+                    nc.gpsimd.tensor_tensor(h[:, cols], plain[:], pingw_rows[:, c, :], ALU.mult)
+                else:
+                    nc.vector.tensor_tensor(h[:, cols], sums[c], pingw_rows[:, c, :], ALU.mult)
+            return h
+
         def make_h(r):
             codes, scales = w1q[r]
             h = held("h%d" % r, [P, S], F32)
+            sums = banks(r % 2)
             for c in range(PING_CHUNKS):
-                sums = bank(c)
                 for jj in range(PACK):
                     cols = slice(jj * P, (jj + 1) * P)
                     nc.tensor.matmul_mx(
-                        out=sums[:, cols],
+                        out=sums[c][:, cols],
                         lhsT=picked_words[c][:, cols].bitcast(FP8X4),
                         lhsT_scale=picked_scales[:, c * BANK + jj * P:c * BANK + (jj + 1) * P],
                         rhs=codes[:].bitcast(FP8X4), rhs_scale=scales[:], start=True, stop=True)
+            for c in range(PING_CHUNKS):
                 weighted = held("weighted%d" % c, [P, BANK], F32)
                 for jj in range(PACK):
                     cols = slice(jj * P, (jj + 1) * P)
                     j_tile = c * PACK + jj
-                    nc.scalar.activation(weighted[:, cols], sums[:, cols], ACT.Copy,
+                    nc.scalar.activation(weighted[:, cols], sums[c][:, cols], ACT.Copy,
                                          scale=columns[:, j_tile:j_tile + 1])
-                back = bank(PING_CHUNKS + c)
                 for jj in range(PACK):
                     cols = slice(jj * P, (jj + 1) * P)
-                    nc.tensor.transpose(back[:, cols], weighted[:, cols], ident[:])
-                nc.scalar.copy(h[:, c * BANK:(c + 1) * BANK], back[:])
+                    nc.tensor.transpose(sums[c][:, cols], weighted[:, cols], ident[:])
+            for c in range(PING_CHUNKS):
+                nc.scalar.copy(h[:, c * BANK:(c + 1) * BANK], sums[c])
             return h
 
         hops = {}
@@ -165,7 +190,7 @@ def tile_list_ping_hop_scores_kernel(
             nc.vector.tensor_tensor(diff[:], h[:].indirect(p1[:]), second[:], ALU.subtract)
             return diff
 
-        def weight_hops(r, diff):
+        def weight_hops(r, diff, hopw_rows):
             engine = nc.vector if r == ROW_TILES - 1 else nc.gpsimd
             hops[r] = held("hops%d" % (r % PACK), [P, PAIRS], F32)
             engine.tensor_tensor(hops[r][:], diff[:], hopw_rows[:], ALU.mult)
@@ -179,17 +204,24 @@ def tile_list_ping_hop_scores_kernel(
             copy(rounded[:].rearrange("p (j t) -> p j t", t=PACK), planes.rearrange("p (t j) -> p j t", t=PACK))
             return rounded
 
+        hopw_rows = None
+        bias = None
         w2w = None
         w2s = None
         kept0 = None
         a2q0 = None
         for r in range(ROW_TILES):
-            h = make_h(r)
+            h = make_h(r) if r else make_first_h()
             if r == 0:
+                hopw_rows = held("hopw_rows", [P, PAIRS], F32, "plain1")
+                nc.sync.dma_start(hopw_rows[:], hopw.partition_broadcast(P))
                 w2w = held("w2w", [P, PASSES, 2 * N], U8, w1_codes_tag(0))
                 nc.sync.dma_start(w2w[:].bitcast(I32), w2_words.rearrange("a p c -> p a c").bitcast(I32))
+                bias = held("bias", [P, N_TILES], F32, "w1_0_scales")
+                with nc.allow_non_contiguous_dma(reason="one value of b for each partition"):
+                    nc.sync.dma_start(bias[:], b.rearrange("(i p) -> p i", p=P))
             if r == 1:
-                prepare_w1(1, w1_codes_tag(1))
+                prepare_w1(1, "w1_bf0", w1_codes_tag(1))
             if r == 2:
                 w2s = held("w2s", [P, PASSES, N], U8, w1_codes_tag(2))
                 nc.gpsimd.memset(w2s[:].bitcast(I32), 0)
@@ -207,7 +239,7 @@ def tile_list_ping_hop_scores_kernel(
                     keep_hops(t, kept0[:, t * KEPT:(t + 1) * KEPT], 0, KEPT)
             if r == 6:
                 a2q0 = quantise("a2_0", round_kept(nc.scalar.copy, "a2_bf0", kept0[:], KEPT, w1_codes_tag(6))[:], KEPT)
-            weight_hops(r, diff)
+            weight_hops(r, diff, hopw_rows)
 
         def products(acc, first_tile, tiles, width, a, moving, j0, start, stop):
             codes, scales = moving
@@ -225,35 +257,46 @@ def tile_list_ping_hop_scores_kernel(
                     rhs=codes[:, cols].bitcast(FP8X4), rhs_scale=scales[:, cols],
                     start=False, stop=stop and u == tiles - 1)
 
-        starts = [sum(KEPT_CHUNKS[:k]) for k in range(len(KEPT_CHUNKS))]
-        accs = {}
-        next_bank = 0
-        for j0, width in zip(starts, KEPT_CHUNKS):
-            tiles = BANK // (2 * width)
-            for first_tile in range(0, N_TILES, tiles):
-                accs[j0, first_tile] = bank(next_bank)
-                next_bank = next_bank + 1
-                products(accs[j0, first_tile], first_tile, tiles, width, 0, a2q0, j0, True, False)
+        width = KEPT_CHUNK
+        tiles = BANK // (2 * width)
+        groups = [(k, first_tile) for k in range(KEPT_CHUNKS) for first_tile in range(0, N_TILES, tiles)]
+        halves = [banks(0), banks(1)]
+        accs = {group: halves[g // PING_CHUNKS][g % PING_CHUNKS] for g, group in enumerate(groups)}
+        for k, first_tile in groups:
+            products(accs[k, first_tile], first_tile, tiles, width, 0, a2q0, k * width, True, False)
 
-        kept1 = held("kept1", [P, PACK * KEPT], F32, "h%d" % (ROW_TILES - 1))
-        out_view = out.rearrange("(i p) j -> p i j", p=P)
-        for j0, width in zip(starts, KEPT_CHUNKS):
-            planes = kept1[:, PACK * j0:PACK * (j0 + width)]
-            for t in range(PACK):
-                keep_hops(PACK + t, planes[:, t * width:(t + 1) * width], j0, width)
-            copy = nc.vector.tensor_copy if j0 == starts[-1] else nc.scalar.copy
-            rounded = round_kept(copy, "a2_bf1_%d" % j0, planes, width)
-            moving = quantise("a2_1_%d" % j0, rounded[:], width)
-            tiles = BANK // (2 * width)
+        last = ROW_TILES - 1
+        plane_tags = ["h%d" % last, "second%d" % (last % 2), "a2_bf1_0", "a2_bf1_1"]
+        rounded = {}
+
+        def finish_chunk(k):
+            moving = quantise("a2_1_%d" % k, rounded[k][:], width)
             for first_tile in range(0, N_TILES, tiles):
-                acc = accs[j0, first_tile]
-                products(acc, first_tile, tiles, width, 1, moving, 0, False, True)
-                bent = held("bent_%d_%d" % (j0, first_tile), [P, tiles, width], F32)
-                for u in range(tiles):
-                    n_tile = S // P + first_tile + u
-                    nc.scalar.activation(bent[:, u, :], acc[:, 2 * u * width:(2 * u + 1) * width], ACT.Tanh,
-                                         bias=columns[:, n_tile:n_tile + 1])
-                result = held("result_%d_%d" % (j0, first_tile), [P, tiles, width], F32)
-                straight = acc[:].rearrange("p (u s w) -> p u s w", s=2, w=width)[:, :, 1, :]
-                nc.vector.tensor_tensor(result[:], straight, bent[:], ALU.add)
-                nc.sync.dma_start(out_view[:, first_tile:first_tile + tiles, j0:j0 + width], result[:])
+                products(accs[k, first_tile], first_tile, tiles, width, 1, moving, 0, False, True)
+
+        for k in range(KEPT_CHUNKS):
+            planes = held("kept1_%d" % k, [P, PACK * width], F32, plane_tags[k])
+            for t in range(PACK):
+                keep_hops(PACK + t, planes[:, t * width:(t + 1) * width], k * width, width)
+            copy = nc.vector.tensor_copy if k == KEPT_CHUNKS - 1 else nc.scalar.copy
+            rounded[k] = round_kept(copy, "a2_bf1_%d" % k, planes[:], width)
+            if k >= 1:
+                finish_chunk(k - 1)
+        finish_chunk(KEPT_CHUNKS - 1)
+
+        out_view = out.rearrange("(i p) j -> p i j", p=P)
+        bent = held("bent", [P, len(groups) * tiles * width], F32, "raw")
+        result = held("result", [P, len(groups) * tiles * width], F32, "pingw_rows")
+        for g, (k, first_tile) in enumerate(groups):
+            acc = accs[k, first_tile]
+            span = slice(g * tiles * width, (g + 1) * tiles * width)
+            for u in range(tiles):
+                n_tile = first_tile + u
+                nc.scalar.activation(bent[:, (g * tiles + u) * width:(g * tiles + u + 1) * width],
+                                     acc[:, 2 * u * width:(2 * u + 1) * width], ACT.Tanh,
+                                     bias=bias[:, n_tile:n_tile + 1])
+            straight = acc.rearrange("p (u s w) -> p u s w", s=2, w=width)[:, :, 1, :]
+            done = result[:, span].rearrange("p (u w) -> p u w", w=width)
+            nc.vector.tensor_tensor(done, straight, bent[:, span].rearrange("p (u w) -> p u w", w=width), ALU.add)
+            queue = nc.scalar if g == len(groups) - 1 else nc.sync
+            queue.dma_start(out_view[:, first_tile:first_tile + tiles, k * width:(k + 1) * width], done)

@@ -67,8 +67,8 @@ def tile_list_ping_hop_scores_kernel(
             nc.sync.dma_start(raw[:], rows.rearrange("(p i) c -> p i c", i=PACK))
             return raw
 
-        def quantise(name, values, columns):
-            codes = held(name + "_codes", [P, columns], U32)
+        def quantise(name, values, columns, tag=None):
+            codes = held(name + "_codes", [P, columns], U32, tag)
             scales = held(name + "_scales", [P, columns], U8)
             nc.vector.quantize_mx(out=codes[:].bitcast(FP8X4), scales=scales[:], in_=values)
             return codes, scales
@@ -113,7 +113,7 @@ def tile_list_ping_hop_scores_kernel(
         columns = held("columns", [P, S // P], F32)
         nc.scalar.copy(columns[:], turned[0][:, 0:S // P])
         spread = banks(0)
-        pingw_rows = held("pingw_rows", [P, PING_CHUNKS, BANK], F32)
+        pingw_rows = held("pingw_rows", [P, PING_CHUNKS, BANK], F32, "raw")
         for c in range(PING_CHUNKS):
             for jj in range(PACK):
                 j_tile = c * PACK + jj
@@ -209,19 +209,17 @@ def tile_list_ping_hop_scores_kernel(
         w2w = None
         w2s = None
         kept0 = None
-        a2q0 = None
         for r in range(ROW_TILES):
             h = make_h(r) if r else make_first_h()
             if r == 0:
-                hopw_rows = held("hopw_rows", [P, PAIRS], F32, "plain1")
+                hopw_rows = held("hopw_rows", [P, PAIRS], F32, "plain0")
                 nc.sync.dma_start(hopw_rows[:], hopw.partition_broadcast(P))
                 w2w = held("w2w", [P, PASSES, 2 * N], U8, w1_codes_tag(0))
                 nc.sync.dma_start(w2w[:].bitcast(I32), w2_words.rearrange("a p c -> p a c").bitcast(I32))
                 bias = held("bias", [P, N_TILES], F32, "w1_0_scales")
                 with nc.allow_non_contiguous_dma(reason="one value of b for each partition"):
                     nc.sync.dma_start(bias[:], b.rearrange("(i p) -> p i", p=P))
-            if r == 1:
-                prepare_w1(1, "w1_bf0", w1_codes_tag(1))
+                prepare_w1(1, "w1_bf0", "w1_bf1")
             if r == 2:
                 w2s = held("w2s", [P, PASSES, N], U8, w1_codes_tag(2))
                 nc.gpsimd.memset(w2s[:].bitcast(I32), 0)
@@ -237,66 +235,63 @@ def tile_list_ping_hop_scores_kernel(
                 kept0 = held("kept0", [P, PACK * KEPT], F32, "h%d" % r)
                 for t in (1, 2, 3, 0):
                     keep_hops(t, kept0[:, t * KEPT:(t + 1) * KEPT], 0, KEPT)
-            if r == 6:
-                a2q0 = quantise("a2_0", round_kept(nc.scalar.copy, "a2_bf0", kept0[:], KEPT, w1_codes_tag(6))[:], KEPT)
             weight_hops(r, diff, hopw_rows)
 
-        def products(acc, first_tile, tiles, width, a, moving, j0, start, stop):
+        last = ROW_TILES - 1
+        rounded0 = round_kept(nc.scalar.copy, "a2_bf0", kept0[:], KEPT, "weighted%d" % (PING_CHUNKS - 1))
+        a2q0 = quantise("a2_0", rounded0[:], KEPT, "diff%d" % (last % 2))
+
+        def products(k, a, moving, j0):
             codes, scales = moving
             cols = slice(j0, j0 + width)
-            for u in range(tiles):
-                n0 = (first_tile + u) * P
-                nc.tensor.matmul_mx(
-                    out=acc[:, 2 * u * width:(2 * u + 1) * width],
-                    lhsT=w2w[:, a, 2 * n0:2 * (n0 + P)].bitcast(FP4X4), lhsT_scale=w2s[:, a, n0:n0 + P],
-                    rhs=codes[:, cols].bitcast(FP8X4), rhs_scale=scales[:, cols],
-                    start=start and u == 0, stop=False)
-                nc.tensor.matmul_mx(
-                    out=acc[:, (2 * u + 1) * width:(2 * u + 2) * width],
-                    lhsT=w3q[a][0][:, n0:n0 + P].bitcast(FP8X4), lhsT_scale=w3q[a][1][:, n0:n0 + P],
-                    rhs=codes[:, cols].bitcast(FP8X4), rhs_scale=scales[:, cols],
-                    start=False, stop=stop and u == tiles - 1)
+            weights = (
+                lambda n0: (w2w[:, a, 2 * n0:2 * (n0 + P)].bitcast(FP4X4), w2s[:, a, n0:n0 + P]),
+                lambda n0: (w3q[a][0][:, n0:n0 + P].bitcast(FP8X4), w3q[a][1][:, n0:n0 + P]),
+            )
+            for acc, weight in zip(accs[k], weights):
+                for i in range(N_TILES):
+                    weight_codes, weight_scales = weight(i * P)
+                    nc.tensor.matmul_mx(
+                        out=acc[:, i * width:(i + 1) * width], lhsT=weight_codes, lhsT_scale=weight_scales,
+                        rhs=codes[:, cols].bitcast(FP8X4), rhs_scale=scales[:, cols],
+                        start=a == 0 and i == 0, stop=a == PASSES - 1 and i == N_TILES - 1)
 
         width = KEPT_CHUNK
-        tiles = BANK // (2 * width)
-        groups = [(k, first_tile) for k in range(KEPT_CHUNKS) for first_tile in range(0, N_TILES, tiles)]
-        halves = [banks(0), banks(1)]
-        accs = {group: halves[g // PING_CHUNKS][g % PING_CHUNKS] for g, group in enumerate(groups)}
-        for k, first_tile in groups:
-            products(accs[k, first_tile], first_tile, tiles, width, 0, a2q0, k * width, True, False)
+        all_banks = banks(0) + banks(1)
+        accs = [all_banks[2 * k:2 * k + 2] for k in range(KEPT_CHUNKS)]
+        for k in range(KEPT_CHUNKS):
+            products(k, 0, a2q0, k * width)
 
-        last = ROW_TILES - 1
         plane_tags = ["h%d" % last, "second%d" % (last % 2), "a2_bf1_0", "a2_bf1_1"]
         rounded = {}
 
         def finish_chunk(k):
-            moving = quantise("a2_1_%d" % k, rounded[k][:], width)
-            for first_tile in range(0, N_TILES, tiles):
-                products(accs[k, first_tile], first_tile, tiles, width, 1, moving, 0, False, True)
+            products(k, 1, quantise("a2_1_%d" % k, rounded[k][:], width), 0)
 
         for k in range(KEPT_CHUNKS):
             planes = held("kept1_%d" % k, [P, PACK * width], F32, plane_tags[k])
             for t in range(PACK):
                 keep_hops(PACK + t, planes[:, t * width:(t + 1) * width], k * width, width)
-            copy = nc.vector.tensor_copy if k == KEPT_CHUNKS - 1 else nc.scalar.copy
-            rounded[k] = round_kept(copy, "a2_bf1_%d" % k, planes[:], width)
             if k >= 1:
                 finish_chunk(k - 1)
+            copy = nc.vector.tensor_copy if k == KEPT_CHUNKS - 1 else nc.scalar.copy
+            rounded[k] = round_kept(copy, "a2_bf1_%d" % k, planes[:], width)
         finish_chunk(KEPT_CHUNKS - 1)
 
         out_view = out.rearrange("(i p) j -> p i j", p=P)
-        bent = held("bent", [P, len(groups) * tiles * width], F32, "raw")
-        result = held("result", [P, len(groups) * tiles * width], F32, "pingw_rows")
-        for g, (k, first_tile) in enumerate(groups):
-            acc = accs[k, first_tile]
-            span = slice(g * tiles * width, (g + 1) * tiles * width)
-            for u in range(tiles):
-                n_tile = first_tile + u
-                nc.scalar.activation(bent[:, (g * tiles + u) * width:(g * tiles + u + 1) * width],
-                                     acc[:, 2 * u * width:(2 * u + 1) * width], ACT.Tanh,
-                                     bias=bias[:, n_tile:n_tile + 1])
-            straight = acc.rearrange("p (u s w) -> p u s w", s=2, w=width)[:, :, 1, :]
-            done = result[:, span].rearrange("p (u w) -> p u w", w=width)
-            nc.vector.tensor_tensor(done, straight, bent[:, span].rearrange("p (u w) -> p u w", w=width), ALU.add)
-            queue = nc.scalar if g == len(groups) - 1 else nc.sync
-            queue.dma_start(out_view[:, first_tile:first_tile + tiles, k * width:(k + 1) * width], done)
+        bent = held("bent", [P, N_TILES * KEPT], F32, "w1_bf0")
+        result = held("result", [P, N_TILES * KEPT], F32, "raw")
+        for k in range(KEPT_CHUNKS):
+            curved, straight = accs[k]
+            base = k * BANK
+            for i in range(N_TILES):
+                nc.scalar.activation(bent[:, base + i * width:base + (i + 1) * width],
+                                     curved[:, i * width:(i + 1) * width], ACT.Tanh, bias=bias[:, i:i + 1])
+            queues = (nc.sync, nc.scalar) if k == KEPT_CHUNKS - 1 else (nc.sync,)
+            tiles = N_TILES // len(queues)
+            for part, queue in enumerate(queues):
+                cols = slice(part * tiles * width, (part + 1) * tiles * width)
+                span = slice(base + cols.start, base + cols.stop)
+                nc.vector.tensor_tensor(result[:, span], straight[:, cols], bent[:, span], ALU.add)
+                queue.dma_start(out_view[:, part * tiles:(part + 1) * tiles, k * width:(k + 1) * width],
+                                result[:, span].rearrange("p (i j) -> p i j", j=width))

@@ -24,6 +24,7 @@ ROW_TILES = H // P
 PASSES = H // (P * PACK)
 PING_CHUNKS = S // BANK
 N_TILES = N // P
+FIRST_PIECES = ((0, 512), (512, 1024), (1024, 1536), (1536, 1792), (1792, 2048))
 KEPT_CHUNK = 128
 KEPT_CHUNKS = KEPT // KEPT_CHUNK
 
@@ -41,9 +42,11 @@ def tile_list_ping_hop_scores_kernel(
         def held(name, shape, dtype, tag=None):
             return sb.tile(shape, dtype, name=name, tag=tag or name, align_bytes=64)
 
-        def banks(parity, count=PING_CHUNKS):
-            names = ["bank%d" % (parity * PING_CHUNKS + c) for c in range(count)]
-            return [psum.tile([P, BANK], F32, name=name, tag=name)[:] for name in names]
+        def bank(index):
+            return psum.tile([P, BANK], F32, name="bank%d" % index, tag="bank%d" % index)[:]
+
+        def banks(parity):
+            return [bank(parity * PING_CHUNKS + c) for c in range(PING_CHUNKS)]
 
         def load_list(name, source):
             tile = lists.tile(list(source.shape), U16, name=name)
@@ -54,8 +57,10 @@ def tile_list_ping_hop_scores_kernel(
         nc.gpsimd.memset(rows[:], 0.0)
         idx = load_list("idx", offs)
         table_scales = held("table_scales", [P, T], U8)
-        nc.sync.dma_start(table_scales[:].bitcast(I32),
-                          tab_scales[0].bitcast(I32).unsqueeze(1).to_broadcast([16, 8, T // 4]))
+        nc.sync.dma_start(table_scales[0:32, :].bitcast(I32),
+                          tab_scales[0].bitcast(I32).unsqueeze(1).to_broadcast([16, 2, T // 4]))
+        nc.vector.memset(table_scales[32:64, :].bitcast(I32), 0)
+        nc.gpsimd.memset(table_scales[64:P, :].bitcast(I32), 0)
         p2 = load_list("p2", pos2)
         p4 = load_list("p4", pos4)
         p1 = load_list("p1", pos1)
@@ -67,8 +72,8 @@ def tile_list_ping_hop_scores_kernel(
             nc.sync.dma_start(raw[:], rows.rearrange("(p i) c -> p i c", i=PACK))
             return raw
 
-        def quantise(name, values, columns, tag=None):
-            codes = held(name + "_codes", [P, columns], U32, tag)
+        def quantise(name, values, columns):
+            codes = held(name + "_codes", [P, columns], U32)
             scales = held(name + "_scales", [P, columns], U8)
             nc.vector.quantize_mx(out=codes[:].bitcast(FP8X4), scales=scales[:], in_=values)
             return codes, scales
@@ -108,10 +113,10 @@ def tile_list_ping_hop_scores_kernel(
 
         ident = held("ident", [P, P], F32)
         make_identity(nc, ident[:])
-        turned = banks(1, 1)
-        nc.tensor.transpose(turned[0][:, 0:P], rows[:], ident[:])
+        turned = bank(PING_CHUNKS)
+        nc.tensor.transpose(turned[:, 0:P], rows[:], ident[:])
         columns = held("columns", [P, S // P], F32)
-        nc.scalar.copy(columns[:], turned[0][:, 0:S // P])
+        nc.scalar.copy(columns[:], turned[:, 0:S // P])
         spread = banks(0)
         pingw_rows = held("pingw_rows", [P, PING_CHUNKS, BANK], F32, "raw")
         for c in range(PING_CHUNKS):
@@ -126,30 +131,34 @@ def tile_list_ping_hop_scores_kernel(
         picked_scales = held("picked_scales", [P, S], U8)
         nc.gpsimd.memset(picked_scales[:].bitcast(I32), 0)
         for q in range(4):
-            nc.sync.dma_start(picked_scales[q:P:32, :].bitcast(I32), gathered_scales[8 * q:P:32, :].bitcast(I32))
+            nc.sync.dma_start(picked_scales[q:P:32, :].bitcast(I32), gathered_scales[2 * q:32:8, :].bitcast(I32))
         picked_words = []
         for c in range(PING_CHUNKS):
             words = held("picked_words%d" % c, [P, BANK], U32)
-            nc.vector.tensor_copy(
-                words[:], table_words[:].bitcast(U32).indirect(idx[:, c * BANK // 16:(c + 1) * BANK // 16]))
+            for j0, j1 in FIRST_PIECES:
+                if j0 // BANK == c:
+                    nc.vector.tensor_copy(words[:, j0 - c * BANK:j1 - c * BANK],
+                                          table_words[:].bitcast(U32).indirect(idx[:, j0 // 16:j1 // 16]))
             picked_words.append(words)
 
         def make_first_h():
             codes, scales = w1q[0]
             h = held("h0", [P, S], F32)
-            sums = banks(0)
-            for c in range(PING_CHUNKS):
-                cols = slice(c * BANK, (c + 1) * BANK)
+            sums = banks(0) + [bank(2 * PING_CHUNKS - 1)]
+            for piece, (j0, j1) in enumerate(FIRST_PIECES):
+                c = j0 // BANK
+                within = slice(j0 - c * BANK, j1 - c * BANK)
+                products = sums[piece][:, 0:j1 - j0]
                 nc.tensor.matmul_mx(
-                    out=sums[c], lhsT=codes[:].bitcast(FP8X4), lhsT_scale=scales[:],
-                    rhs=picked_words[c][:].bitcast(FP8X4), rhs_scale=picked_scales[:, cols],
+                    out=products, lhsT=codes[:].bitcast(FP8X4), lhsT_scale=scales[:],
+                    rhs=picked_words[c][:, within].bitcast(FP8X4), rhs_scale=picked_scales[:, j0:j1],
                     start=True, stop=True)
                 if c < PING_CHUNKS // 2:
                     plain = held("plain%d" % c, [P, BANK], F32)
-                    nc.scalar.copy(plain[:], sums[c])
-                    nc.gpsimd.tensor_tensor(h[:, cols], plain[:], pingw_rows[:, c, :], ALU.mult)
+                    nc.scalar.copy(plain[:], products)
+                    nc.gpsimd.tensor_tensor(h[:, j0:j1], plain[:], pingw_rows[:, c, :], ALU.mult)
                 else:
-                    nc.vector.tensor_tensor(h[:, cols], sums[c], pingw_rows[:, c, :], ALU.mult)
+                    nc.vector.tensor_tensor(h[:, j0:j1], products, pingw_rows[:, c, within], ALU.mult)
             return h
 
         def make_h(r):
@@ -209,6 +218,7 @@ def tile_list_ping_hop_scores_kernel(
         w2w = None
         w2s = None
         kept0 = None
+        a2q0 = None
         for r in range(ROW_TILES):
             h = make_h(r) if r else make_first_h()
             if r == 0:
@@ -235,11 +245,12 @@ def tile_list_ping_hop_scores_kernel(
                 kept0 = held("kept0", [P, PACK * KEPT], F32, "h%d" % r)
                 for t in (1, 2, 3, 0):
                     keep_hops(t, kept0[:, t * KEPT:(t + 1) * KEPT], 0, KEPT)
+            if r == 6:
+                rounded0 = round_kept(nc.scalar.copy, "a2_bf0", kept0[:], KEPT, w1_codes_tag(6))
+                a2q0 = quantise("a2_0", rounded0[:], KEPT)
             weight_hops(r, diff, hopw_rows)
 
         last = ROW_TILES - 1
-        rounded0 = round_kept(nc.scalar.copy, "a2_bf0", kept0[:], KEPT, "weighted%d" % (PING_CHUNKS - 1))
-        a2q0 = quantise("a2_0", rounded0[:], KEPT, "diff%d" % (last % 2))
 
         def products(k, a, moving, j0):
             codes, scales = moving

from contextlib import ExitStack

import concourse.mybir as mybir
from concourse.masks import make_identity

K, T, S, PAIRS, KEPT, H, N = 512, 4096, 2048, 1024, 512, 1024, 512
FLOPS = 2 * K * H * S + 2 * 2 * H * N * KEPT

F32 = mybir.dt.float32
BF16 = mybir.dt.bfloat16
I32 = mybir.dt.int32
U32 = mybir.dt.uint32
U16 = mybir.dt.uint16
U8 = mybir.dt.uint8
FP8X4 = mybir.dt.float8_e4m3fn_x4
FP4X4 = mybir.dt.float4_e2m1fn_x4
ALU = mybir.AluOpType
ACT = mybir.ActivationFunctionType

P = 128
PACK = 4
BANK = 512
ROW_TILES = H // P
PASSES = H // (P * PACK)
PING_CHUNKS = S // BANK
N_TILES = N // P
FIRST_PIECES = ((0, 512), (512, 1024), (1024, 1536), (1536, 1792), (1792, 2048))
KEPT_CHUNK = 128
KEPT_CHUNKS = KEPT // KEPT_CHUNK


def tile_list_ping_hop_scores_kernel(
    tc, tab_words, tab_scales, offs, pos1, pos2, pos3, pos4, w1, pingw, hopw,
    w2_words, w2_scales, b, w3, out,
):
    nc = tc.nc
    with ExitStack() as ctx:
        lists = ctx.enter_context(tc.tile_pool(name="lists", bufs=1))
        sb = ctx.enter_context(tc.tile_pool(name="sb", bufs=1))
        psum = ctx.enter_context(tc.psum_pool(name="psum", bufs=1))

        def held(name, shape, dtype, tag=None):
            return sb.tile(shape, dtype, name=name, tag=tag or name, align_bytes=64)

        def bank(index):
            return psum.tile([P, BANK], F32, name="bank%d" % index, tag="bank%d" % index)[:]

        def banks(parity):
            return [bank(parity * PING_CHUNKS + c) for c in range(PING_CHUNKS)]

        def load_list(name, source):
            tile = lists.tile(list(source.shape), U16, name=name)
            nc.sync.dma_start(tile[:], source)
            return tile

        rows = held("rows", [P, P], F32)
        nc.gpsimd.memset(rows[:], 0.0)
        idx = load_list("idx", offs)
        table_scales = held("table_scales", [P, T], U8)
        nc.sync.dma_start(table_scales[0:32, :].bitcast(I32),
                          tab_scales[0].bitcast(I32).unsqueeze(1).to_broadcast([16, 2, T // 4]))
        nc.vector.memset(table_scales[32:64, :].bitcast(I32), 0)
        nc.gpsimd.memset(table_scales[64:P, :].bitcast(I32), 0)
        p2 = load_list("p2", pos2)
        p4 = load_list("p4", pos4)
        p1 = load_list("p1", pos1)
        p3 = load_list("p3", pos3)
        nc.sync.dma_start(rows[0:S // P, :], pingw.rearrange("(c p) -> c p", p=P))

        def load_raw(rows, tag):
            raw = held("raw", [P, PACK, BANK], F32, tag)
            nc.sync.dma_start(raw[:], rows.rearrange("(p i) c -> p i c", i=PACK))
            return raw

        def quantise(name, values, columns):
            codes = held(name + "_codes", [P, columns], U32)
            scales = held(name + "_scales", [P, columns], U8)
            nc.vector.quantize_mx(out=codes[:].bitcast(FP8X4), scales=scales[:], in_=values)
            return codes, scales

        def w1_codes_tag(tile_index):
            return "w1_%d_codes" % tile_index

        w1q = {}

        def prepare_w1(half, raw_tag, tag):
            raw = load_raw(w1[:, half * BANK:(half + 1) * BANK], raw_tag)
            rounded = held("w1_bf%d" % half, [P, BANK * PACK], BF16, tag)
            src = raw[:].rearrange("p i (m t) -> p m t i", t=PACK)
            dst = rounded[:].rearrange("p (t m i) -> p m t i", t=PACK, i=PACK)
            for piece in range(2):
                ms = slice(piece * P // 2, (piece + 1) * P // 2)
                nc.scalar.copy(dst[:, ms], src[:, ms])
            for t in range(PACK):
                tile_index = half * PACK + t
                w1q[tile_index] = quantise("w1_%d" % tile_index, rounded[:, t * BANK:(t + 1) * BANK], P)

        w3q = {}

        def prepare_w3(a, tag):
            raw = load_raw(w3[a * BANK:(a + 1) * BANK, :], "w1_bf0")
            rounded = held("w3_bf%d" % a, [P, N * PACK], BF16, tag)
            src = raw[:].rearrange("p i n -> p n i")
            dst = rounded[:].rearrange("p (n i) -> p n i", i=PACK)
            for piece in range(2):
                ns = slice(piece * N // 2, (piece + 1) * N // 2)
                nc.scalar.copy(dst[:, ns], src[:, ns])
            w3q[a] = quantise("w3_%d" % a, rounded[:], N)

        prepare_w1(0, "raw", "w1_bf0")
        table_words = held("table_words", [P, T], I32)
        nc.sync.dma_start(table_words[:], tab_words[0].rearrange("p t i -> p (t i)").bitcast(I32))

        ident = held("ident", [P, P], F32)
        make_identity(nc, ident[:])
        turned = bank(PING_CHUNKS)
        nc.tensor.transpose(turned[:, 0:P], rows[:], ident[:])
        columns = held("columns", [P, S // P], F32)
        nc.scalar.copy(columns[:], turned[:, 0:S // P])
        spread = banks(0)
        pingw_rows = held("pingw_rows", [P, PING_CHUNKS, BANK], F32, "raw")
        for c in range(PING_CHUNKS):
            for jj in range(PACK):
                j_tile = c * PACK + jj
                nc.tensor.transpose(spread[c][:, jj * P:(jj + 1) * P],
                                    columns[:, j_tile:j_tile + 1].to_broadcast([P, P]), ident[:])
            nc.scalar.copy(pingw_rows[:, c, :], spread[c])

        gathered_scales = held("gathered_scales", [P, S], U8)
        nc.vector.tensor_copy(gathered_scales[:], table_scales[:].indirect(idx[:]))
        picked_scales = held("picked_scales", [P, S], U8)
        nc.gpsimd.memset(picked_scales[:].bitcast(I32), 0)
        for q in range(4):
            nc.sync.dma_start(picked_scales[q:P:32, :].bitcast(I32), gathered_scales[2 * q:32:8, :].bitcast(I32))
        picked_words = []
        for c in range(PING_CHUNKS):
            words = held("picked_words%d" % c, [P, BANK], U32)
            for j0, j1 in FIRST_PIECES:
                if j0 // BANK == c:
                    nc.vector.tensor_copy(words[:, j0 - c * BANK:j1 - c * BANK],
                                          table_words[:].bitcast(U32).indirect(idx[:, j0 // 16:j1 // 16]))
            picked_words.append(words)

        def make_first_h():
            codes, scales = w1q[0]
            h = held("h0", [P, S], F32)
            sums = banks(0) + [bank(2 * PING_CHUNKS - 1)]
            for piece, (j0, j1) in enumerate(FIRST_PIECES):
                c = j0 // BANK
                within = slice(j0 - c * BANK, j1 - c * BANK)
                products = sums[piece][:, 0:j1 - j0]
                nc.tensor.matmul_mx(
                    out=products, lhsT=codes[:].bitcast(FP8X4), lhsT_scale=scales[:],
                    rhs=picked_words[c][:, within].bitcast(FP8X4), rhs_scale=picked_scales[:, j0:j1],
                    start=True, stop=True)
                if c < PING_CHUNKS // 2:
                    plain = held("plain%d" % c, [P, BANK], F32)
                    nc.scalar.copy(plain[:], products)
                    nc.gpsimd.tensor_tensor(h[:, j0:j1], plain[:], pingw_rows[:, c, :], ALU.mult)
                else:
                    nc.vector.tensor_tensor(h[:, j0:j1], products, pingw_rows[:, c, within], ALU.mult)
            return h

        def make_h(r):
            codes, scales = w1q[r]
            h = held("h%d" % r, [P, S], F32)
            sums = banks(r % 2)
            for c in range(PING_CHUNKS):
                for jj in range(PACK):
                    cols = slice(jj * P, (jj + 1) * P)
                    nc.tensor.matmul_mx(
                        out=sums[c][:, cols],
                        lhsT=picked_words[c][:, cols].bitcast(FP8X4),
                        lhsT_scale=picked_scales[:, c * BANK + jj * P:c * BANK + (jj + 1) * P],
                        rhs=codes[:].bitcast(FP8X4), rhs_scale=scales[:], start=True, stop=True)
            for c in range(PING_CHUNKS):
                weighted = held("weighted%d" % c, [P, BANK], F32)
                for jj in range(PACK):
                    cols = slice(jj * P, (jj + 1) * P)
                    j_tile = c * PACK + jj
                    nc.scalar.activation(weighted[:, cols], sums[c][:, cols], ACT.Copy,
                                         scale=columns[:, j_tile:j_tile + 1])
                for jj in range(PACK):
                    cols = slice(jj * P, (jj + 1) * P)
                    nc.tensor.transpose(sums[c][:, cols], weighted[:, cols], ident[:])
            for c in range(PING_CHUNKS):
                nc.scalar.copy(h[:, c * BANK:(c + 1) * BANK], sums[c])
            return h

        hops = {}
        alibis = {}

        def make_hops(r, h):
            second = held("second%d" % (r % 2), [P, PAIRS], F32)
            nc.vector.tensor_copy(second[:], h[:].indirect(p2[:]))
            alibis[r] = held("alibi%d" % r, [P, KEPT], F32)
            nc.vector.tensor_copy(alibis[r][:], h[:].indirect(p4[:]))
            diff = held("diff%d" % (r % 2), [P, PAIRS], F32)
            nc.vector.tensor_tensor(diff[:], h[:].indirect(p1[:]), second[:], ALU.subtract)
            return diff

        def weight_hops(r, diff, hopw_rows):
            engine = nc.vector if r == ROW_TILES - 1 else nc.gpsimd
            hops[r] = held("hops%d" % (r % PACK), [P, PAIRS], F32)
            engine.tensor_tensor(hops[r][:], diff[:], hopw_rows[:], ALU.mult)

        def keep_hops(r, dst, j0, width):
            nc.vector.tensor_tensor(dst, hops[r][:].indirect(p3[:, j0 // 16:(j0 + width) // 16]),
                                    alibis[r][:, j0:j0 + width], ALU.add)

        def round_kept(copy, name, planes, width, tag=None):
            rounded = held(name, [P, width * PACK], BF16, tag)
            copy(rounded[:].rearrange("p (j t) -> p j t", t=PACK), planes.rearrange("p (t j) -> p j t", t=PACK))
            return rounded

        hopw_rows = None
        bias = None
        w2w = None
        w2s = None
        kept0 = None
        a2q0 = None
        for r in range(ROW_TILES):
            h = make_h(r) if r else make_first_h()
            if r == 0:
                hopw_rows = held("hopw_rows", [P, PAIRS], F32, "plain0")
                nc.sync.dma_start(hopw_rows[:], hopw.partition_broadcast(P))
                w2w = held("w2w", [P, PASSES, 2 * N], U8, w1_codes_tag(0))
                nc.sync.dma_start(w2w[:].bitcast(I32), w2_words.rearrange("a p c -> p a c").bitcast(I32))
                bias = held("bias", [P, N_TILES], F32, "w1_0_scales")
                with nc.allow_non_contiguous_dma(reason="one value of b for each partition"):
                    nc.sync.dma_start(bias[:], b.rearrange("(i p) -> p i", p=P))
                prepare_w1(1, "w1_bf0", "w1_bf1")
            if r == 2:
                w2s = held("w2s", [P, PASSES, N], U8, w1_codes_tag(2))
                nc.gpsimd.memset(w2s[:].bitcast(I32), 0)
                for q in range(4):
                    nc.sync.dma_start(w2s[32 * q:32 * q + 4].bitcast(I32),
                                      w2_scales[:, 4 * q:4 * q + 4, :].rearrange("a q c -> q a c").bitcast(I32))
            if r == 4:
                prepare_w3(0, w1_codes_tag(4))
            if r == 7:
                prepare_w3(1, w1_codes_tag(7))
            diff = make_hops(r, h)
            if r == PACK:
                kept0 = held("kept0", [P, PACK * KEPT], F32, "h%d" % r)
                for t in (1, 2, 3, 0):
                    keep_hops(t, kept0[:, t * KEPT:(t + 1) * KEPT], 0, KEPT)
            if r == 6:
                rounded0 = round_kept(nc.scalar.copy, "a2_bf0", kept0[:], KEPT, w1_codes_tag(6))
                a2q0 = quantise("a2_0", rounded0[:], KEPT)
            weight_hops(r, diff, hopw_rows)

        last = ROW_TILES - 1

        def products(k, a, moving, j0):
            codes, scales = moving
            cols = slice(j0, j0 + width)
            weights = (
                lambda n0: (w2w[:, a, 2 * n0:2 * (n0 + P)].bitcast(FP4X4), w2s[:, a, n0:n0 + P]),
                lambda n0: (w3q[a][0][:, n0:n0 + P].bitcast(FP8X4), w3q[a][1][:, n0:n0 + P]),
            )
            for acc, weight in zip(accs[k], weights):
                for i in range(N_TILES):
                    weight_codes, weight_scales = weight(i * P)
                    nc.tensor.matmul_mx(
                        out=acc[:, i * width:(i + 1) * width], lhsT=weight_codes, lhsT_scale=weight_scales,
                        rhs=codes[:, cols].bitcast(FP8X4), rhs_scale=scales[:, cols],
                        start=a == 0 and i == 0, stop=a == PASSES - 1 and i == N_TILES - 1)

        width = KEPT_CHUNK
        all_banks = banks(0) + banks(1)
        accs = [all_banks[2 * k:2 * k + 2] for k in range(KEPT_CHUNKS)]
        for k in range(KEPT_CHUNKS):
            products(k, 0, a2q0, k * width)

        plane_tags = ["h%d" % last, "second%d" % (last % 2), "a2_bf1_0", "a2_bf1_1"]
        rounded = {}

        def finish_chunk(k):
            products(k, 1, quantise("a2_1_%d" % k, rounded[k][:], width), 0)

        for k in range(KEPT_CHUNKS):
            planes = held("kept1_%d" % k, [P, PACK * width], F32, plane_tags[k])
            for t in range(PACK):
                keep_hops(PACK + t, planes[:, t * width:(t + 1) * width], k * width, width)
            if k >= 1:
                finish_chunk(k - 1)
            copy = nc.vector.tensor_copy if k == KEPT_CHUNKS - 1 else nc.scalar.copy
            rounded[k] = round_kept(copy, "a2_bf1_%d" % k, planes[:], width)
        finish_chunk(KEPT_CHUNKS - 1)

        out_view = out.rearrange("(i p) j -> p i j", p=P)
        bent = held("bent", [P, N_TILES * KEPT], F32, "w1_bf0")
        result = held("result", [P, N_TILES * KEPT], F32, "raw")
        for k in range(KEPT_CHUNKS):
            curved, straight = accs[k]
            base = k * BANK
            for i in range(N_TILES):
                nc.scalar.activation(bent[:, base + i * width:base + (i + 1) * width],
                                     curved[:, i * width:(i + 1) * width], ACT.Tanh, bias=bias[:, i:i + 1])
            queues = (nc.sync, nc.scalar) if k == KEPT_CHUNKS - 1 else (nc.sync,)
            tiles = N_TILES // len(queues)
            for part, queue in enumerate(queues):
                cols = slice(part * tiles * width, (part + 1) * tiles * width)
                span = slice(base + cols.start, base + cols.stop)
                nc.vector.tensor_tensor(result[:, span], straight[:, cols], bent[:, span], ALU.add)
                queue.dma_start(out_view[:, part * tiles:(part + 1) * tiles, k * width:(k + 1) * width],
                                result[:, span].rearrange("p (i j) -> p i j", j=width))
